import numpy as np, ml_dtypes
CORES = [40,41,42,43,44,45,46,47]
N = 8
BF = ml_dtypes.bfloat16
def gentries(a):
    return np.ascontiguousarray(a.reshape(8, 16, -1).transpose(0, 2, 1)).reshape(8, -1)
def gtable(e):
    e = np.asarray(e); return np.ascontiguousarray(e.reshape(8, -1, 16).transpose(0, 2, 1)).reshape(128, -1).astype(np.int32)
W, T, L, RO = 2560, 320, 6, 3
R = W >> 7
def chain(par, a):
    c = [a]
    for i in range(L - 1): c.append(np.take_along_axis(par, c[-1], 1))
    return np.stack(c, axis=1)
def meeting(ca, cb):
    eq = (ca[:, :, None] == cb[:, None]).reshape(8, L * L, T)
    found = np.any(eq, axis=1); first = np.argmax(eq, axis=1); i = first // L
    return found, np.where(found, i, 0), np.where(found, first - L * i, 0)
def one_round(f, par, a, b, own):
    ca, cb = chain(par, a), chain(par, b); found, I, J = meeting(ca, cb)
    pos = np.arange(L)[None, :, None]
    both = np.concatenate([ca, cb], axis=1); on = np.concatenate([pos < I[:, None], pos < J[:, None]], axis=1)
    mine = np.take_along_axis(own, both.reshape(8, -1), 1).reshape(8, 2 * L, T) == np.arange(T)
    kept = np.all(mine | ~on, axis=1)
    v = np.take_along_axis(f, both.reshape(1, 8, 1, -1), 3).reshape(N, 8, 16, 2 * L, T)
    sg = np.repeat(np.array([1, -1]), L)[:, None]
    D = np.sum(v * (sg * on)[None, :, None], axis=3, keepdims=True)
    n = (I + J + 1)[None, :, None, None]
    votes = np.sum((n * v <= sg * D) & on[None, :, None], axis=(0, 2))
    place = np.where(votes > 8 * N, np.tile(np.arange(L), 2)[:, None], -1)
    ka, kb = np.max(place[:, :L], axis=1), np.max(place[:, L:], axis=1)
    side = ka < 0; k = np.where(side, kb, ka); go = kept & found & (k >= 0); k = np.maximum(k, 0)
    s3 = side[:, None]; s5 = side[None, :, None, None]
    P, Q = np.where(s3, cb, ca), np.where(s3, ca, cb); X, Y = np.where(side, J, I), np.where(side, I, J)
    vp, vq = np.where(s5, v[:, :, :, L:], v[:, :, :, :L]), np.where(s5, v[:, :, :, :L], v[:, :, :, L:])
    M = np.take_along_axis(vp, k[None, :, None, None], 3)
    before = np.concatenate([np.zeros_like(M), vp[:, :, :, :-1]], axis=3)
    turn = pos <= k[:, None]
    newp = np.where(turn[None, :, None], M - before, vp - M); newq = vq + M
    g3 = go[:, None]
    to = np.concatenate([np.where(g3 & (pos < X[:, None]), P, W), np.where(g3 & (pos < Y[:, None]), Q, W)], axis=1)
    f2 = np.concatenate([f, np.zeros((N, 8, 16, 1), f.dtype)], axis=3)
    np.put_along_axis(f2, to.reshape(1, 8, 1, -1), np.concatenate([newp, newq], axis=3).reshape(N, 8, 16, -1), 3)
    p2 = np.concatenate([par, np.zeros((8, 1), par.dtype)], axis=1)
    np.put_along_axis(p2, np.where(g3 & turn, P, W).reshape(8, -1), np.concatenate([Q[:, :1], P[:, :-1]], axis=1).reshape(8, -1), 1)
    na = np.where(go, np.take_along_axis(P, k[:, None], 1)[:, 0], a)
    nb = np.where(go, np.take_along_axis(P, np.minimum(k + 1, L - 1)[:, None], 1)[:, 0], b)
    return f2[..., :W], p2[:, :W], na, nb
def forest(rng, q, ends):
    x = np.arange(W)
    pp = np.where(rng.random((8, W)) < q, x - R, x - 1 - (rng.random((8, W)) * np.minimum(x, 3 * R)).astype(np.int64)); pp[:, :R] = x[:R]
    lab = np.argsort(rng.random((8, W)), axis=1)
    if ends:
        for g in range(8):
            for at, num in ((W - 1, 0), (0, W - 1)):
                j = int(np.argmax(lab[g] == num)); lab[g, j] = lab[g, at]; lab[g, at] = num
    return pp, lab
def flows(rng, pp, lab):
    base = np.where(rng.random((W, 8, 1, 1)) < 0.55, np.exp2(6 * rng.random((W, 8, 1, 1))), 0)
    c = (2 * base * rng.random((W, 8, N, 16))).astype(np.int64); ar = np.arange(8)
    for x in range(W - 1, R - 1, -1): c[pp[:, x], ar] += c[x]
    f = np.zeros((N, 8, 16, W), np.int64)
    np.put_along_axis(f, lab[None, :, None], np.minimum(c, 4095).transpose(2, 1, 3, 0), 3)
    return f
def lay(rng, p, lo, spoil, fix=(), hold=()):
    kids = [[] for v in range(W)]
    for v in range(W):
        if p[v] != v: kids[p[v]].append(v)
    leaf = np.array([not c for c in kids])
    o = np.argsort(rng.random(W) + np.where(~leaf & (rng.random(W) < 0.7), 1.0, 0.0)); o = np.concatenate([np.array([0, W - 1]), o[(o != 0) & (o != W - 1)]])
    wi = np.where(rng.random(W) < 0.06, L, rng.integers(lo, L, W)); wj = np.where(rng.random(W) < 0.06, L, rng.integers(lo - 1, L, W))
    num = rng.permutation(T).tolist(); own = rng.integers(0, T, W).tolist(); a, b = rng.integers(0, W, (2, T)); free = [True] * W; made = 0
    for y in hold: free[y] = False
    tops = [v for v in range(W) if p[v] == v]; tops = [tops[i] for i in rng.permutation(len(tops))]; low = []
    for v in tops[:2 * (len(tops) // 4)]:
        for s in range(int(rng.integers(0, L))):
            if kids[v]: v = kids[v][int(rng.integers(0, len(kids[v])))]
        low.append(v)
    pairs = [(u, v) for u, v in fix] + [(u, v) for u, v in zip(low[::2], low[1::2])]
    for u, v in pairs:
        cu, cv = [u], [v]
        for s in range(L - 1):
            cu.append(p[cu[-1]]); cv.append(p[cv[-1]])
        i = next((s for s in range(L) if cu[s] in cv), L); j = cv.index(cu[i]) if i < L else L
        z = num[made]; made += 1; a[z] = u; b[z] = v
        for y in cu[:i] + cv[:j]:
            free[y] = False; own[y] = z
    for v, i, j in zip(o.tolist(), wi.tolist(), wj.tolist()):
        if made >= 15 * T // 16: break
        if not free[v] or p[v] == v: continue
        up = [v]; dn = []; x = p[v]
        while len(up) < i and free[x] and p[x] != x:
            up.append(x); x = p[x]
        while len(dn) < j:
            c = [y for y in kids[x] if free[y] and y != up[-1]]
            if not c: break
            c = [y for y in c if kids[y]] or c
            x = c[made % len(c)]; dn.append(x)
        z = num[made]; made += 1; a[z] = v; b[z] = x
        for y in up + dn:
            free[y] = False; own[y] = z
        if spoil > 0 and rng.random() < (0.5 if z >= T - 2 else spoil):
            near = z >= T - 2 or rng.random() < 0.5
            own[(up + dn)[int(rng.integers(0, len(up) + len(dn)))]] = z ^ 1 if near else (z + 1 + int(rng.integers(0, T - 1))) % T
    for i, z in enumerate(num[made:]):
        x = int(a[z])
        if i % 4 == 0: b[z] = x
        if i % 4 == 1:
            for s in range(1 + (i >> 2) % L): x = p[x]
            b[z] = x
        if i % 4 == 2:
            c = kids[p[p[x]]]
            if c: b[z] = c[i % len(c)]
    sw = rng.random(T) < 0.5; sw[np.array(num[:len(pairs)], np.int64)] = False
    return np.where(sw, b, a), np.where(sw, a, b), np.array(own)
def numbered(rng, up, fp, fix, hold):
    lab = rng.permutation(W); par = np.zeros(W, np.int64); par[lab] = lab[np.array(up)]
    f = np.zeros((N, 16, W), np.int64); f[:, :, lab] = fp
    return par, f, [[(int(lab[u]), int(lab[v])) for u, v in x] for x in fix], [int(lab[y]) for y in hold]
def beads(rng, line=False):
    most = L - 1 if line else 2 * (L - 1); total = min(W - 1, most * T); n = total // T + (np.arange(T) < total % T).astype(np.int64)
    o = rng.permutation(T); x, y = o[:T // 2], o[T // 2:]
    d = (rng.random(T // 2) * (np.minimum(most - n[x], n[y] - 1) + 1)).astype(np.int64); n[x] += d; n[y] -= d
    gap = np.bincount(rng.integers(0, T, W - 1 - total), minlength=T).tolist(); n = n.tolist()
    fp = rng.integers(0, 4096, (N, 16, W)); up = [0]; x = 0; fix = []
    for j in range(T):
        i = n[j] if line else int(rng.integers(max(0, n[j] - L + 1), min(n[j], L - 1) + 1)); br = []
        for c in (i, n[j] - i):
            y = x; z = []
            for s in range(c):
                up.append(y); y = len(up) - 1; z.append(y)
            br.append(z)
        A, B = br; fix.append((A[-1] if A else x, B[-1] if B else x))
        P, Q = (A, B) if len(A) >= len(B) else (B, A)
        fp[:, :, P] = rng.integers(2048, 4096, (N, 16, len(P)))
        if Q: fp[:, :, Q] = rng.integers(0, min(4095, 2048 * (len(P) - 1) // len(Q)) + 1, (N, 16, len(Q)))
        who = (rng.permutation(16 * N) < int(rng.integers(8 * N + 1, 16 * N + 1))).reshape(N, 16)
        m = P[int(rng.integers(0, len(P)))]; fp[:, :, m] = np.where(who, 0, fp[:, :, m]); x = P[-1]
        for s in range(gap[j]):
            up.append(x); x = len(up) - 1
    return numbered(rng, up, fp, [fix] + [[] for t in range(RO - 1)], [])
def straight(rng):
    return beads(rng, True)
def heavy(rng):
    S = L - 1; top = ((L - 2) * 4000 - 4095) // L; light = ((L - 2) * 4095 // S + (L - 2) * (top + 3995) // S) // 2
    up = [0]; fp = rng.integers(0, 4096, (N, 16, W)); fix = [[] for t in range(RO)]
    def put(at, lo, hi):
        up.append(at); fp[:, :, len(up) - 1] = rng.integers(lo, hi + 1, (N, 16))
        return len(up) - 1
    def lift(at, m, weak):
        q = put(at, light - 520, light - 480) if weak else put(at, 4045, 4095); y = at; P = []
        for s in range(S - 1, -1, -1):
            y = put(y, 4000, 4095) if s != m else put(y, 500, 500) if weak else put(y, top - 50, top)
            P.append(y)
        fix[0].append((y, q))
        return q, P[::-1]
    x = 0
    for u in range(16):
        x = put(x, 0, 4095); y1 = put(x, 0, 0); y0 = put(y1, 4000, 4095); fix[0].append((y0, x))
        weak = int(rng.integers(0, S)); y = x
        for i in range(S): y = lift(y, int(rng.integers(0, S)), u % 2 == 1 and i == weak)[0]
        fix[1].append((y, x if u % 2 == 1 else y1))
    if RO > 2:
        for u in range(8):
            x = put(x, 0, 4095); y1 = put(x, 0, 0); y0 = put(y1, 4000, 4095); fix[0].append((y0, x))
            q, P = lift(y0, 1, False); q2 = lift(y1, int(rng.integers(0, S)), False)[0]; q1 = lift(q2, int(rng.integers(0, S)), False)[0]
            fix[1].append((P[1], y0)); fix[1].append((q1, y0)); fix[2].append((P[0], y1))
    hold = [y for y in range(len(up))]
    while len(up) < W: up.append(len(up) - 1 - int(rng.random() * min(len(up), 3 * R)))
    return numbered(rng, up, fp, fix, hold)
def draw(rng, q=0.7, lo=1, spoil=0.12, ends=False, change=None, plant=None, still=False, make=()):
    pp, lab = forest(rng, q, ends); par = np.zeros((8, W), np.int64); np.put_along_axis(par, lab, np.take_along_axis(lab, pp, 1), 1)
    f = flows(rng, pp, lab) if change is None else change(rng)
    ts = []; rs = []; quiet = rng.permutation(8).tolist(); one = int(rng.integers(0, T))
    fix = [[[] for t in range(RO)] for g in range(8)]; hold = [[] for g in range(8)]
    for g, m in zip(quiet[2:], make):
        par[g], f[:, g], fix[g], hold[g] = m(rng)
    now = par
    for t in range(RO):
        z = [lay(rng, now[g].tolist(), lo, spoil, fix[g][t], hold[g]) for g in range(8)]
        a, b, own = [np.stack([y[i] for y in z]) for i in range(3)]
        if still:
            b[quiet[0]] = a[quiet[0]]; own[quiet[1]] = one
        if t == 0:
            if plant is not None: f = plant(rng, f, now, a, b, own)
            f0 = f
        ts.append(np.concatenate([a, b], axis=1)); rs.append(own)
        if t < RO - 1: f, now, a, b = one_round(f, now, a, b, own)
    return {"fl": np.ascontiguousarray(f0.reshape(N, 128, W)).astype(np.float32), "par": np.stack([par] * N).astype(np.int32),
            "tie": np.stack([gtable(np.concatenate(ts, axis=1))] * N), "res": np.stack([np.concatenate(rs, axis=1)] * N).astype(np.int32)}
def exact_votes(rng, f, par, a, b, own):
    f = f.copy(); ca, cb = chain(par, a), chain(par, b); found, I, J = meeting(ca, cb)
    for g in range(8):
        for j in range(T):
            X, Y = int(I[g, j]), int(J[g, j]); P, Q = ca[g, :X, j], cb[g, :Y, j]
            if X + Y == 0 or np.any(own[g, P] != j) or np.any(own[g, Q] != j): continue
            if X == 0 or (Y > 0 and rng.random() < 0.5): X, Y, P, Q = Y, X, Q, P
            m = int(rng.integers(0, X)); z = int(m > 0 and rng.random() < 0.5)
            h = int(rng.integers(1, 4095 // (X + Y) + 1)); top = (X - 1 - z) * h
            c = (8 * N - 1, 8 * N, 8 * N + 1, 8 * N + 2, 0, 16 * N)[(g + j) % 6]
            who = (rng.permutation(16 * N) < c).reshape(N, 16)
            if rng.random() < 0.5: who = rng.permuted((np.arange(16 * N) < c).reshape(N, 16)[rng.permutation(N)], axis=1)
            less = top - rng.integers(0, top + 1, (N, 16)) * rng.integers(0, 2, (N, 16))
            f[:, g, :, P] = (X + Y) * h; f[:, g, :, Q] = 0
            if z: f[:, g, :, int(P[m - 1])] = 0
            f[:, g, :, int(P[m])] = np.where(who, less, top + 1)
    return f
def few(rng):
    vals = np.array([0, 0, 0, 1, 2, 4095]); k = rng.choice(vals, (1, 8, 1, W))
    return np.where(rng.random((N, 8, 16, W)) < 0.15, rng.choice(vals, (N, 8, 16, W)), k)
def uneven(rng):
    return np.minimum((np.exp2(12 * rng.random((1, 8, 1, W))) * rng.random((N, 8, 16, W))).astype(np.int64), 4095)
def setup_inputs(rng):
    return draw(rng)
def setup_inputs_votes(rng):
    return draw(rng, spoil=0.05, plant=exact_votes)
def setup_inputs_ends(rng):
    return draw(rng, q=0.85, lo=L - 1, ends=True, make=(straight, beads))
def setup_inputs_flat(rng):
    return draw(rng, change=few, make=(heavy,))
def setup_inputs_still(rng):
    return draw(rng, q=0.6, spoil=0.0, still=True)
def setup_inputs_spread(rng):
    return draw(rng, q=0.75, change=uneven)
def check_inputs(d):
    bad = []
    for k, lo, hi in (("fl", 0, 4095), ("par", 0, W - 1), ("tie", 0, W - 1), ("res", 0, T - 1)):
        if not (np.min(d[k]) >= lo and np.max(d[k]) <= hi): bad.append("range of " + k)
    if np.any(d["fl"] != np.floor(d["fl"])): bad.append("whole numbers in fl")
    for k in ("par", "tie", "res"):
        if np.any(d[k] != d[k][:1]): bad.append(k + " alike on all ranks")
    if "range of par" not in bad:
        p = d["par"].astype(np.int64).reshape(-1, W); q = p
        for i in range(12): q = np.take_along_axis(q, q, 1)
        if np.any(np.take_along_axis(p, q, 1) != q): bad.append("every bus has a root")
    return bad
def reference(fl, par, tie, res):
    f = fl.astype(np.int64).reshape(N, 8, 16, W); p = par[0].astype(np.int64)
    e = gentries(tie[0]).astype(np.int64).reshape(8, RO, 2, T); own = res[0].astype(np.int64).reshape(8, RO, W); new = np.zeros_like(e)
    for t in range(RO):
        f, p, na, nb = one_round(f, p, e[:, t, 0], e[:, t, 1], own[:, t])
        new[:, t, 0] = na; new[:, t, 1] = nb
    return {"yf": f.reshape(N, 128, W).astype(np.float32), "yp": np.stack([p] * N).astype(np.float32), "yt": np.stack([gtable(new.reshape(8, -1))] * N).astype(np.float32)}

from concourse.bass import DstId, RemoteDMATransfer
from concourse.mybir import AluOpType as A, ActivationFunctionType as F

SIM_CORES = 64
NB = 2560
KP = 112
BL = 16 * KP
F0 = 16
RS = 4 * BL + 8 * KP
WC = F0 + NB + 2 * RS + 4 * BL
LCM = 27720.0
SL = 296
O_L, O_V, O_M, O_F, O_P = 0, 120, 168, 192, 256

f32, bf, i32, u16 = "float32", "bfloat16", "int32", "uint16"
SCRATCH = {}
for _d, _l in (
    (f32, dict(W=[WC], YF=[NB], Y2=[NB], tab=[NB], SC=[2 * BL], ones=[384], idn=[128], nid=[128], id3=[8, 16], id21=[6, 21], Z=[240],
               selc=[384], selx=[30], grp=[8], m16=[16], pf=[8], cf=[48], tif=[6, 21], y0=[6, 3], GX=[KP], GY=[96],
               CH=[48], CH3=[6, 6], TB=[6, 5, 5], E2=[288], NE=[288], NS=[288], r48=[288], r12=[36], k12=[36], k5=[30], k10=[60],
               N6=[6, 6], MT=[6, 6], GD=[36], AG=[36], SN=[36], rn=[8], JN=[30], LOC=[6, 5], NSL=[30], VAL=[30], VA7=[30], TH=[30],
               thc=[3, 2, 5], UI=[30], DMP=[32], DP=[6, 5], D2=[6, 5], VD=[30], NI=[6, 5], SLY=[32], SLE=[512], DQ=[3, 6, 5],
               DK=[2, 6, 5], QM=[90], QS=[90], ENDS=[2, 3], EN=[6, 21], VF=[120], VA=[96], OK=[30], TF=[30], GO=[4],
               LF=[4, 8, 16], CF=[24], C1=[KP], XS=[4 * KP], EM=[2, 8, 16], BS=[84], BT=[84], PFI=[160], EFI=[128],
               YP=[256], PR=[256], YT=[120])),
    (bf, dict(DW=[3008], CMP=[30 * KP], SP=[2, 448], idb=[128], gb=[16], bsel=[8, 16], acol=[4], C4=[5, 30], C2=[30, 2], ph=[2],
              V=[32, 16], VS=[448])),
    (i32, dict(tab0=[NB], ii=[40], pi=[8], tii=[120], TT=[3, 2, 5], pr0=[256])),
    (u16, dict(LAND=[8, SL], VSND=[3, 128], lst=[40], x0=[3, 8], ofx=[8], ofy=[8], ofs=[28], OFF=[320], OFM=[56])),
):
    for _k, _s in _l.items():
        SCRATCH[_k] = ("sbuf", [128] + _s, _d)
for _k in range(8):
    SCRATCH["P%d" % _k] = ("psum", [128, 512], f32)
SEMAPHORES = ["cv", "ca", "ct", "cp", "sent", "dtie", "dtab", "dfl", "dpr", "dout", "hand"] + ["x%d" % _k for _k in range(10)]


def helper_of(c, T, topo):
    for o in range(SIM_CORES):
        if topo.same_plane(topo.chip(o), topo.chip(c)):
            return topo.cores_of(o)[topo.cores_of(c).index(c)]


def to(c, topo):
    rid, pid, _ = topo.addr(c)
    return DstId(rid=rid, pnc=pid)


def hand_on(g, core, T, topo):
    for r, c in enumerate(T.cores):
        if helper_of(c, T, topo) == core:
            ap = T.LAND[:, r, O_P:O_P + 36]
            others = [o for o in T.cores if o != c]
            g.wait_ge(T.sem.hand, len(topo.engines(c, core)))
            g.remote_dma_fused([RemoteDMATransfer(dst_ids=[to(o, topo) for o in others], dma_engine_mask=topo.mask(core, c),
                                                  remote_sem=T.sem.x9, src=ap, dsts=[ap] * len(others))], local_sem=T.sem.sent)
            g.wait_ge(T.sem.sent, len(topo.engines(core, c)))


def rank_program(g, core, T, topo):
    me = T.rank_of(core)
    if me is None:
        hand_on(g, core, T, topo)
        return
    Q = {"v": g.vector, "a": g.scalar, "t": g.tensor, "p": g, "s": g.sync}
    cnt = {"v": 0, "a": 0, "t": 0, "p": 0}
    waited, lastw, readers, dcount = {}, {}, {}, {}

    def wait(e, tok):
        s, n = tok
        if waited.get((e, s), 0) < n:
            waited[(e, s)] = n
            Q[e].wait_ge(T.sem[s], n)

    def deps(e, rd, wr):
        own = "c" + e
        for k in rd:
            if k in lastw and not (e == "t" and lastw[k][0] == own):
                wait(e, lastw[k])
            if k[0] == "P":
                for s, n in readers.get(k, {}).items():
                    if s != own:
                        wait(e, (s, n))
        for k in wr:
            if k in lastw and not (lastw[k][0] == own and (e == "t" or k[0] == "P")):
                wait(e, lastw[k])
            for s, n in readers.get(k, {}).items():
                if not (s == own and (e == "t" or k[0] == "P")):
                    wait(e, (s, n))

    def note(tok, rd, wr):
        for k in rd:
            readers.setdefault(k, {})[tok[0]] = tok[1]
        for k in wr:
            lastw[k] = tok
            readers[k] = {}

    def op(e, fn, rd, wr):
        rd, wr = rd.split(), wr.split()
        deps(e, rd, wr)
        cnt[e] += 1
        fn().then_inc(T.sem["c" + e], 1)
        note(("c" + e, cnt[e]), rd, wr)

    def done(k, e="v"):
        lastw[k] = ("c" + e, cnt[e])
        readers[k] = {}

    v, a, pe = g.vector, g.scalar, g.tensor

    def cp(o, i, rd, wr, e="v"):
        op(e, (lambda: v.tensor_copy(o, i)) if e == "v" else (lambda: a.activation(o, i, F.Copy)), rd, wr)

    def sca(o, i, s, rd, wr):
        op("a", lambda: a.activation(o, i, F.Copy, scale=s), rd, wr)

    def tt(o, x, y, f, rd, wr):
        op("v", lambda: v.tensor_tensor(o, x, y, f), rd, wr)

    def ts(o, x, s1, f, rd, wr, s2=None, f2=None):
        op("v", (lambda: v.tensor_scalar(o, x, s1, None, f)) if f2 is None else (lambda: v.tensor_scalar(o, x, s1, s2, f, f2)), rd, wr)

    def ms(o, c, wr):
        op("v", lambda: v.memset(o, c), "", wr)

    def scan(o, d0, d1, init, f0, f1, rd, wr):
        op("v", lambda: v.tensor_tensor_scan(o, d0, d1, init, f0, f1), rd, wr)

    def mm(o, l, r, rd, wr, st=True, sp=True):
        op("t", lambda: pe.matmul(o, l, r, st, sp), rd, wr)

    def iota(o, pat, base, cm, wr):
        op("p", lambda: g.iota(o, pat, base, cm, allow_small_or_imprecise_dtypes=True), "", wr)

    def sel(o, i, pat, base, cm, wr):
        op("p", lambda: g.affine_select(o, i, pat, A.is_equal, 0.0, base, cm), "ones", wr)

    def dma(e, o, i, sem, rd, wr):
        rd, wr = rd.split(), wr.split()
        deps(e, rd, wr)
        dcount[sem] = dcount.get(sem, 0) + 16
        Q[e].dma_start(o, i).then_inc(T.sem[sem], 16)
        note((sem, dcount[sem]), rd, wr)

    peers = [r for r in range(len(T.cores)) if r != me]
    eng = topo.engines(core, T.cores[peers[0]])
    sent = [0]

    def bcast(off, n, x, rd):
        deps("p", rd.split(), [])
        ap = T.LAND[:, me, off:off + n]
        g.remote_dma_fused([RemoteDMATransfer(dst_ids=[to(T.cores[r], topo) for r in peers], dma_engine_mask=topo.mask(core, T.cores[peers[0]]),
                                              remote_sem=T.sem[x], src=ap, dsts=[ap] * len(peers))], local_sem=T.sem.sent)
        sent[0] += len(eng)
        lastw[x] = (x, len(eng) * len(peers))

    def votes_out(t, x):
        deps("p", ["VSND"], [])
        w = len(eng) // len(T.cores)
        tr = []
        for n, r in enumerate(peers):
            tr.append(RemoteDMATransfer(dst_ids=[to(T.cores[r], topo)], dma_engine_mask=sum(1 << e for e in eng[n * w:(n + 1) * w]),
                                        remote_sem=T.sem[x], src=T.VSND[:, t, 15 * r:15 * r + 15],
                                        dst=T.LAND[:, me, O_V + 16 * t:O_V + 16 * t + 15]))
        g.remote_dma_fused(tr, local_sem=T.sem.sent)
        sent[0] += w * len(peers)
        lastw[x] = (x, w * len(peers))

    P = [T["P%d" % k] for k in range(8)]
    Y = slice(0, KP)
    W, CH, CH3, TB, LAND = T.W, T.CH, T.CH3, T.TB, T.LAND
    add, sub, mul = A.add, A.subtract, A.mult

    def ub(t):
        return F0 + NB + t * RS

    dma("s", T.tii[0:16, :], T.tie[16 * me:16 * me + 16, :], "dtie", "", "tii")
    ms(T.ones[:, :], 1.0, "ones")
    ms(T.tab0[:, 0:1888], 0, "tab0")
    iota(T.tab0[:, 1888:NB], [[0, NB - 1888]], 0, 0, "tab0b")
    sel(T.Z[0:16, :], T.ones[0:16, 0:240], [[1, 240]], -112, -1, "Z")
    sel(T.idn[:, :], T.ones[:, 0:128], [[-1, 128]], 0, 1, "idn")
    iota(T.pi[:, 0:1], [[0, 1]], 0, 1, "pi")
    iota(T.ii[:, 0:18], [[8, 6], [2, 3]], 0, 0, "ii0")
    iota(T.ii[:, 18:36], [[16, 3], [-8, 2], [0, 3]], 8, 0, "ii1")
    iota(T.cf[:, 16:46], [[16, 3], [0, 10]], 0, 3, "cf1")
    iota(T.cf[:, 0:16], [[1, 16]], 0, 0, "cf0")
    iota(T.UI[:, :], [[1, 30]], 0, 16, "UI")
    iota(T.DMP[:, :], [[KP, 4], [0, 8]], NB, 1, "DMP")
    iota(T.BS[:, 0:32], [[1280, 2], [1, 16]], F0, 16, "BS0")
    sel(T.selc[0:24, :], T.ones[0:24, :], [[-1, 3], [-3, 8], [0, 16]], 0, 1, "selc")
    deps("s", [], ["tab0", "tab0b"])
    deps("a", [], ["tab0", "tab0b"])
    for h in range(7):
        dma("sa"[h % 2], T.tab0[16 * h:16 * h + 1, :], T.par[me:me + 1, :], "dtab", "", "")
    for h in range(6):
        dma("as"[h % 2], T.tab0[16 * h + 2:16 * h + 5, :], T.res[me:me + 1, :], "dtab", "", "")
    lastw["tab0"] = ("dtab", dcount["dtab"])
    dma("s", W[:, F0:F0 + NB], T.fl[:, :], "dfl", "", "f0")
    for b in range(2):
        dma("s", T.pr0[0:80, 128 * b:128 * b + 128], T.par[4 * b:4 * b + 4, :], "dpr", "", "")
    lastw["pr0"] = ("dpr", 32)

    ms(T.tif[0:16, :, 20], 0.0, "tifp")
    cp(T.tif[0:16, :, 0:20], T.tii[0:16, :], "tii", "tif")
    for h in range(6):
        mm(P[5][:, 0:21], T.Z[0:16, 112 - 16 * h:240 - 16 * h], T.tif[0:16, (1 - h % 2)::2, (h // 2)::3], "Z tif tifp", "P5", h == 0, h == 5)
    for c in range(7):
        mm(P[6][:, 0:18], T.Z[0:16, 112 - 16 * c:240 - 16 * c], T.tif[0:16, :, 3 * c:3 * c + 3], "Z tif tifp", "P6", c == 0, c == 6)
    ms(CH[:, :], 0.0, "CH")
    ms(T.ofx[:, :], 0, "ofx")
    ms(T.ofy[:, :], 0, "ofy")
    ms(LAND[:, me, :], 0, "own")
    ms(T.r48[:, :], 0.0, "r48")
    ms(T.r12[:, :], 0.0, "r12")
    ms(T.k12[:, :], 1.0, "k12")
    ms(T.MT[:, :, :], 0.0, "MT")
    ms(T.r48[:, 0::48], 1.0, "r48")
    ms(T.r12[:, 0::12], 1.0, "r12")
    ms(T.k12[:, 0::12], 0.0, "k12")
    cp(T.id3[:, :, :], T.idn[:, :], "idn", "id3", "a")
    cp(T.selx[:, :], T.id3[:, 0:6, 0:5], "id3", "selx", "a")
    ts(T.pi[:, 1:2], T.pi[:, 0:1], 15, A.bitwise_and, "pi", "pi1")
    ts(T.pi[:, 2:3], T.pi[:, 0:1], 4, A.arith_shift_right, "pi", "pi2")
    ts(T.pi[:, 3:4], T.pi[:, 0:1], 7, A.bitwise_and, "pi", "pi3")
    ts(T.pi[:, 4:5], T.pi[:, 1:2], 3, A.arith_shift_right, "pi1", "pi4")
    cp(T.pf[:, 0:5], T.pi[:, 0:5], "pi pi1 pi2 pi3 pi4", "pf")
    cp(T.x0[:, :, 0:7], P[5][:, 0:21], "P5", "x0")
    ts(T.pf[:, 5:6], T.pf[:, 3:4], 5.0, A.min, "pf", "pf5")
    ts(T.pf[:, 6:7], T.pf[:, 1:2], -2.0, mul, "pf", "pf6")
    ts(T.lst[:, 0:18], T.ii[:, 0:18], T.pf[:, 4:5], add, "ii0 pf", "l1")
    ts(T.lst[:, 18:36], T.ii[:, 18:36], T.pf[:, 5:6], add, "ii1 pf5", "l2")
    ts(T.JN[:, :], T.cf[:, 16:46], T.pf[:, 6:7], add, "cf1 pf6", "JN")
    cp(T.y0[:, :, :], P[6][:, 0:18], "P6", "y0")

    def consts():
        ms(T.LF[:, 1, :, :], 0.0, "LF1")
        ms(W[:, 0:F0], 0.0, "w0")
        ts(T.grp[:, :], T.cf[:, 0:8], T.pf[:, 2:3], A.is_equal, "cf0 pf", "grp")
        for b, i, c in ((0, 0, 0.0), (0, 5, -1.0), (0, 10, 0.0), (0, 15, -1.0), (1, 0, 0.0), (1, 4, 0.0), (1, 9, -1.0)):
            op("v", lambda: v.memset(T.SP[:, b, i::16], c), "SP", "")
        done("SP")
        cp(T.gb[:, 0:8], T.grp[:, :], "grp", "gb0", "a")
        sca(T.gb[:, 8:16], T.grp[:, :], 256.0, "grp", "gb1")
        ms(T.VSND[:, :, :], 0, "VSND")
        cp(T.tab[:, 1536:NB], T.tab0[:, 1536:NB], "tab0", "tab_3 tab_4")
        ms(T.V[:, :, :], 0.0, "V")
        ts(T.m16[:, :], T.cf[:, 0:16], T.pf[:, 1:2], A.is_equal, "cf0 pf", "m16")
        cp(T.SLY[:, :], T.DMP[:, :], "DMP", "SLY", "a")
        sca(T.nid[:, :], T.idn[:, :], -1.0, "idn", "nid")
        cp(T.idb[:, :], T.idn[:, :], "idn", "idb", "a")
        cp(T.id21[:, :, :], T.idn[:, 0:126], "idn", "id21", "a")
        sca(T.EM[:, :, :, :], T.ones[:, 0:256], 0.0, "ones", "EM0 EM1 EM2 EM3")
        cp(T.k5[:, :], T.ones[:, 0:30], "ones", "k5", "a")
        cp(T.k10[:, :], T.ones[:, 0:60], "ones", "k10", "a")
        sca(T.bsel[:, :, :], T.ones[:, 0:128], 0.0, "ones", "bsel")
        sca(T.thc[:, :, 0, :], T.ones[:, 0:15], 65.0 * 256, "ones", "thc0")
        sca(T.thc[:, :, 1, :], T.ones[:, 0:15], 65.0, "ones", "thc1")
        sca(T.k5[:, 0::5], T.ones[:, 0:6], 0.0, "ones", "k5")
        sca(T.k10[:, 0::10], T.ones[:, 0:6], 0.0, "ones", "k10")
        sca(T.BS[:, 32:64], T.ones[:, 0:32], 0.0, "ones", "BS2")
        sca(T.BS[:, 64:84], T.ones[:, 0:20], 4096.0, "ones", "BS1")
        for t in range(2):
            for b, i in ((0, 4), (0, 9), (0, 14), (1, 3), (1, 8), (1, 13), (1, 14), (1, 15)):
                at = ub(t) + BL * (2 + b)
                sca(W[:, at + i:at + BL:16], T.ones[:, 0:KP], 0.0, "ones", "")
            done("Z%d" % t, "a")
        ts(T.UI[:, 16:30], T.UI[:, 16:30], float(BL - 16), add, "UI", "UI")
        ts(T.acol[:, 0:1], T.pf[:, 1:2], 2.0, A.is_lt, "pf", "ac0")
        ts(T.pf[:, 7:8], T.pf[:, 1:2], 6.0, A.is_lt, "pf", "pf7")
        ms(T.D2[:, :, :], float(2 * BL - 1), "D2")
        ts(T.rn[:, 7:8], T.pf[:, 0:1], 56.0, A.is_ge, "pf", "rn7", float(6 - 896), mul)
        tt(T.acol[:, 1:2], T.pf[:, 7:8], T.acol[:, 0:1], sub, "pf7 ac0", "ac1")
        ms(T.D2[:, 3, 1:2], float(2 * BL - 1 - (BL - 16)), "D2")
        ts(T.bsel[:, :, 0], T.ones[:, 0:8], T.acol[:, 0:1], mul, "ones ac0 bsel", "bse0")
        ts(T.bsel[:, :, 1], T.ones[:, 0:8], T.acol[:, 1:2], mul, "ones ac1 bsel", "bse1")
        for h in range(6):
            rel = 5 * h if h < 4 else 5 * h + BL - 16
            ts(T.D2[:, h, 0:1], T.rn[:, 7:8], float(4 * BL + (h // 2) + 3 * (1 - h % 2) - rel), add, "rn7 D2", "")
        done("D2")
        cp(T.C4[:, 2, :], T.D2[:, :, :], "D2", "C42")
        ts(T.acol[:, 3:4], T.pf[:, 1:2], 4.0, A.is_ge, "pf", "ac3")
        ts(T.pf[:, 7:8], T.pf[:, 1:2], 4.0, A.is_lt, "pf", "pf7")
        tt(T.C4[:, 3, :], T.D2[:, :, :], T.C4[:, 2, :], sub, "C42 D2", "C43")
        cp(T.DK[:, 0, :, :], T.ones[:, 0:30], "ones", "DK", "a")
        sca(T.DK[:, 1, :, :], T.ones[:, 0:30], 0.0, "ones", "DKb")
        sca(T.C4[:, 4, :], T.ones[:, 0:30], float(-2 * BL), "ones", "C44")
        sca(T.DK[:, 0, :, 0], T.cf[:, 0:6], 5.0, "cf0", "DK")
        sca(T.DK[:, 1, 4:6, 0], T.ones[:, 0:2], float(BL - 16), "ones", "DKb")
        sca(T.DK[:, 1, 3, 1:2], T.ones[:, 0:1], float(BL - 16), "ones", "DKb")
        ts(T.rn[:, 3:4], T.pf[:, 0:1], 16.0, mul, "pf", "rn3", float(ub(2)), add)
        tt(T.acol[:, 2:3], T.pf[:, 7:8], T.acol[:, 0:1], sub, "pf7 ac0", "ac2")
        tt(T.NI[:, :, :], T.D2[:, :, :], T.UI[:, :], add, "D2 UI", "NI")
        cp(T.ph[:, 0:1], T.rn[:, 3:4], "rn3", "ph0")
        ms(T.NI[:, :, 0], float(-ub(2)), "NI")
        tt(T.ph[:, 1:2], T.rn[:, 3:4], T.ph[:, 0:1], sub, "rn3 ph0", "ph1")

    TABK = "tab_0 tab_1 tab_2 tab_3 tab_4"
    CHK = "CH CH0 CH0b CH1 CH2 CH3 CH4 CH5"
    TBK = "TB0 TB1 TB2 TB3 TB4"
    TFK = " TF TF0 TF1 TF2"
    VK = " VAL0 VAL1 VAL2"
    C3 = "c3a c3b"

    def wkeys(t):
        return "w0 f0 " + " ".join("U%d N%d Z%d M%d" % (s, s, s, s) for s in range(t))

    def m_recv(t):
        x = "x%d ownM" % (6 + t)
        src = LAND[Y, :, O_M + 8 * t:O_M + 8 * t + 3]
        for hf in range(2):
            ts(T.EM[Y, hf, :, 6 * hf:6 * hf + 3], src, -32768.0, add, x, "EM%d" % (2 * hf))
            ts(T.EM[Y, hf, :, 6 * hf + 3:6 * hf + 6], src, -1.0, mul, x, "EM%d" % (2 * hf + 1), 32768.0, add)
        for hf in range(2):
            mm(P[0][:, 0:56], T.EM[Y, hf, :, :], T.idn[Y, 56 * hf:56 * hf + 56], "EM0 EM1 EM2 EM3 idn", "P0", hf == 0, hf == 1)

    def m_signed(t):
        mb = ub(t) + 4 * BL
        for G in range(3):
            for hf in range(2):
                o = mb + 6 * hf + G
                out = P[1][:, KP * G + 56 * hf:KP * G + 56 * hf + 56]
                mm(out, T.idn[:, :], W[:, o:mb + 896:16], "M%d idn" % t, "P1", True, False)
                mm(out, T.nid[:, :], W[:, o + 3:mb + 896:16], "M%d nid" % t, "P1", False, True)

    def update(t):
        for q in range(30):
            G, s, at = q // 10, q // 5 % 2, ub(t) + BL * (q // 16)
            col = W[:, at + q % 16:at + BL:16]
            tt(col, col, P[1][:, KP * G:KP * G + KP], sub if s else add, "P1", "uq%d" % q)
            if q % 5 < 4:
                sca(W[:, at + 2 * BL + q % 16:at + 3 * BL:16], col, -1.0, "uq%d" % q, "")
        done("U%d" % t)
        done("N%d" % t, "a")

    def chains(t):
        tabw, tk = (T.tab0, "tab0") if t == 0 else (T.tab, TABK)

        def keep(m, e):
            k = 5 if m % 2 == 0 else 7
            cp(CH[Y, m + 1::8], P[k][Y, 0:30:5], "P%d" % k, "CH%d" % (m + 1), e)
            cp(TB[Y, :, :, m], P[k][Y, 0:30], "P%d" % k, "TB%d" % m, e)

        for m in range(5):
            ox, okx = (T.x0[:, t, 0:7], "x0") if m == 0 else (T.ofx[:, 0:7], "ofx")
            k = 5 if m % 2 == 0 else 7
            cp(T.GX[:, :], tabw[:, :].indirect(ox), tk + " " + okx, "GX")
            if m < 4:
                cp(T.GY[:, :], tabw[:, :].indirect(T.ofy[:, 0:6]), tk + " ofy", "GY", "v" if t == 0 else "a")
            if m > 0:
                keep(m - 1, "a")
            if t > 0 and m == 4:
                mb = ub(t - 1) + 4 * BL
                cp(W[:, mb:mb + 896], W[:, 0:ub(t - 1)].indirect(T.OFM[:, :]), "OFM " + wkeys(t - 1), "M%d" % (t - 1), "a")
            if m < 4:
                mm(P[6][0:96, 0:7], T.GY[:, :], T.idn[:, 0:112:16], "GY idn", "P6")
            mm(P[k][Y, 0:30], T.GX[:, :], T.selx[:, :], "GX selx", "P%d" % k)
            if t > 0 and m == 2:
                m_recv(t - 1)
            if t > 0 and m == 3:
                cp(T.OFM[:, :], P[0][:, 0:56], "P0", "OFM")
            if m < 4:
                cp(T.ofx[0:96, 0:7], P[6][0:96, 0:7], "P6", "ofx")
            if m < 3:
                cp(T.ofy[Y, 0:6], P[k][Y, 0:30:5], "P%d" % k, "ofy")
        keep(4, "v")

    def first_ends(t):
        cp(CH[Y, 8::16], T.y0[Y, 2 * t, :], "y0 CH", "CH0", "a")
        cp(CH[Y, 0::16], T.y0[Y, 2 * t + 1, :], "y0 CH", "CH0b", "a")
        cp(T.ofy[Y, 0:6], CH[Y, 0::8], "CH0 CH0b", "ofy")

    def turn_over(r1, n):
        for b in range(2):
            for i in range(16):
                j = 16 * b + i
                mm(P[3][0:80, j:j + 32 * n:32], T.DW[:, 1280 * b + i:1280 * (b + 1):16], T.acol[:, r1:r1 + n], "DW ac1 ac2 ac3", "P3")
        for c in range(20):
            mm(P[4][:, c:c + 1], T.DW[:, 128 * c:128 * c + 128], T.acol[:, 0:1], "DW ac0", "P4")

    def meeting(t):
        if t > 0:
            cp(T.E2[:, :], CH[:, :].indirect(T.lst[:, 18:36]), CHK + " l2", "E2a E2b")
            m_signed(t - 1)
        else:
            cp(T.E2[:, 0:160], CH[:, :].indirect(T.lst[:, 18:28]), CHK + " l2", "E2a", "a")
            cp(T.E2[:, 160:288], CH[:, :].indirect(T.lst[:, 28:36]), CHK + " l2", "E2b")
        tt(T.MT[Y, :, 0:5], TB[Y, :, 2 + t, :], T.JN[Y, :], A.is_equal, TBK + " JN", "MT")
        tt(T.NE[:, :], CH[:, :].indirect(T.lst[:, 0:18]), T.E2[:, :], A.not_equal, CHK + " l1 E2a E2b", "NE")
        cp(CH3[Y, :, 0], CH[Y, 0::8], "CH0 CH0b", "c3a")
        scan(T.NS[Y, :], T.r48[Y, :], T.NE[Y, :], 1.0, A.max, A.min, "NE r48", "NS")
        cp(CH3[Y, :, 1:6], TB[Y, :, 0, :], TBK, "c3b")
        tt(T.GD[Y, :], T.NS[Y, 7::8], T.MT[Y, :, :], A.is_le, "NS MT", "GD")
        scan(T.SN[Y, :], T.k12[Y, :], T.NS[Y, 7::8], 0.0, mul, add, "NS k12", "SN")
        tt(T.LOC[Y, :, :], TB[Y, :, 1, :], CH3[Y, :, 0:5], add, TBK + " " + C3, "LOC")
        scan(T.AG[Y, :], T.r12[Y, :], T.GD[Y, :], 1.0, A.max, A.min, "GD r12", "AG")
        ts(T.rn[Y, 0:3], T.SN[Y, 11::12], 1.0, add, "SN", "rn0")
        ts(T.LOC[Y, :, :], T.LOC[Y, :, :], float(F0), add, "LOC", "LOC")
        cp(T.N6[Y, :, :], T.NS[Y, 7::8], "NS", "N6")
        op("v", lambda: v.reciprocal(T.rn[Y, 4:7], T.rn[Y, 0:3]), "rn0", "rn4")
        tt(T.NSL[Y, :], T.N6[Y, :, 0:5], T.LOC[Y, :, :], mul, "N6 LOC", "NSL")
        o = O_L + 40 * t
        ts(LAND[Y, me, o + 30:o + 33], T.rn[Y, 4:7], LCM, mul, "rn4 own", "ownL3")
        for G in range(3):
            ts(LAND[Y, me, o + 10 * G:o + 10 * G + 10], T.NSL[Y, 10 * G:10 * G + 10], T.AG[Y, 12 * G + 11:12 * G + 12], mul,
               "NSL AG own", "ownL%d" % G)
        bcast(o, 33, "x%d" % t, "ownL0 ownL1 ownL2 ownL3")
        if t > 0:
            turn_over(1, 1)
        iota(T.DW[:, :], [[0, 3008]], 0, 0, "DW")

    def prepare(t):
        for G in range(3):
            ts(T.VAL[Y, 10 * G:10 * G + 10], T.N6[Y, 2 * G:2 * G + 2, 0:5], T.AG[Y, 12 * G + 11:12 * G + 12], mul, "N6 AG", "VAL%d" % G)
        tt(T.SLY[Y, 0:30], CH3[Y, :, 0:5], T.DMP[Y, 0:30], sub, C3 + " DMP", "SLY")
        tt(T.VD[Y, :], T.UI[Y, :] if t < 2 else T.NI[Y, :, :], T.LOC[Y, :, :], sub, "UI NI LOC", "VD")
        ts(T.TH[Y, :], T.VAL[Y, :], -1.0e6, mul, VK, "TH", 1.0e6, add)
        tt(T.SLY[Y, 0:30], T.SLY[Y, 0:30], T.VAL[Y, :], mul, "SLY" + VK, "SLY")
        ts(T.VD[Y, :], T.VD[Y, :], float(ub(t)), add, "VD", "VD")
        tt(T.TH[Y, :], T.TH[Y, :], T.thc[Y, :, :, :], add, "TH thc0 thc1", "TH")
        tt(T.SLY[Y, 0:30], T.SLY[Y, 0:30], T.DMP[Y, 0:30], add, "SLY DMP", "SLY")
        if t < 2:
            tt(T.VD[Y, :], T.VD[Y, :], T.VAL[Y, :], mul, "VD" + VK, "VD")
        deps("a", [], ["SLE"])
        for i in range(16):
            sca(T.SLE[Y, i::16], T.SLY[Y, :], T.m16[Y, i:i + 1], "SLY m16", "")
        done("SLE", "a")
        tt(T.DP[Y, :, 1:5], CH3[Y, :, 0:4], CH3[Y, :, 2:6], sub, C3, "DP0")
        tt(T.DP[Y, 0::2, 0], CH3[Y, 1::2, 0], CH3[Y, 0::2, 1], sub, C3, "DP1")
        tt(T.DP[Y, 1::2, 0], CH3[Y, 0::2, 0], CH3[Y, 1::2, 1], sub, C3, "DP2")
        hi, lo, kh, kl = (T.C2[Y, :, 0], T.C2[Y, :, 1], "C20", "C21") if t < 2 else (T.C4[Y, 2, :], T.C4[Y, 3, :], "C42", "C43")
        cp(hi, T.VD[Y, :], "VD", kh)
        for k in range(4):
            mm(P[7][:, 7 * k:7 * k + 7], T.SLE[Y, 128 * k:128 * k + 128], T.grp[Y, 0:7], "SLE grp", "P7")
        cp(T.C4[Y, 0, :], T.DP[Y, :, :], "DP0 DP1 DP2", "C40")
        tt(lo, T.VD[Y, :], hi, sub, "VD " + kh, kl)
        tt(T.C4[Y, 1, :], T.DP[Y, :, :], T.C4[Y, 0, :], sub, "DP0 DP1 DP2 C40", "C41")
        if t < 2:
            tt(T.DQ[Y, 0, 1::2, 1:5], T.LOC[Y, 1::2, 1:5], T.LOC[Y, 1::2, 0:4], sub, "LOC", "DQ0")
            tt(T.DQ[Y, 0, 0::2, 1:5], T.LOC[Y, 0::2, 0:4], T.LOC[Y, 0::2, 1:5], sub, "LOC", "DQ1")
            cp(T.DQ[Y, 0, 1::2, 0], T.LOC[Y, 1::2, 0], "LOC", "DQ2", "a")
            sca(T.DQ[Y, 0, 0::2, 0], T.LOC[Y, 0::2, 0], -1.0, "LOC", "DQ3")
            first_ends(t + 1)
        else:
            for r in range(2):
                ts(T.C2[Y, :, r], T.VAL[Y, :], T.ph[Y, r:r + 1], mul, "ph0 ph1" + VK, "C2%d" % r)
            ts(T.VA7[Y, :], T.VAL[Y, :], float(2 * BL), mul, VK, "VA7")
            u = ub(2)
            sca(W[:, u + 2 * BL:u + 4 * BL], W[:, u:u + 2 * BL], -1.0, "u0 u1 u2 u3 u4 u5 u6 u7", "N2")
        if t > 0:
            ends(t - 1)
        else:
            ts(T.PR[0:80, :], T.pr0[0:80, :], -4096.0, add, "pr0", "PR")
        tt(T.DQ[Y, 1, :, 1:5], CH3[Y, :, 1:5], CH3[Y, :, 0:4], sub, C3, "DQ4")
        tt(T.DQ[Y, 2, :, 1:5], CH3[Y, :, 2:6], CH3[Y, :, 1:5], sub, C3, "DQ5")
        for s in range(2):
            tt(T.DQ[Y, 1, s::2, 0], CH3[Y, s::2, 0], CH3[Y, 1::2, 0], sub, C3, "DQ6%d" % s)
            tt(T.DQ[Y, 2, s::2, 0], CH3[Y, s::2, 1], CH3[Y, 0::2, 0], sub, C3, "DQ7%d" % s)
        cp(T.ofs[:, :], P[7][:, 0:28], "P7", "ofs")

    def ends(t):
        tt(T.QM[Y, 30:60], T.DQ[Y, 1, :, :], T.TF[Y, :], mul, "DQ4 DQ60 DQ61" + TFK, "QM1")
        tt(T.QM[Y, 60:90], T.DQ[Y, 2, :, :], T.TF[Y, :], mul, "DQ5 DQ70 DQ71" + TFK, "QM2")
        scan(T.QS[Y, 30:90], T.k10[Y, :], T.QM[Y, 30:90], 0.0, mul, add, "QM1 QM2 k10", "QS1")
        tt(T.ENDS[Y, :, :], T.QS[Y, 39:90:10], T.y0[Y, 2 * t:2 * t + 2, :], add, "QS1 y0", "ENDS")
        for c in range(7):
            if t == 1:
                ts(T.EN[Y, 2 * t:2 * t + 2, 3 * c:3 * c + 3], T.ENDS[Y, :, :], T.grp[Y, c:c + 1], mul, "ENDS grp", "")
            else:
                sca(T.EN[Y, 2 * t:2 * t + 2, 3 * c:3 * c + 3], T.ENDS[Y, :, :], T.grp[Y, c:c + 1], "ENDS grp", "")
        done("EN%d" % t, "v" if t == 1 else "a")

    def worker(t):
        x, o, u = "x%d ownL0 ownL1 ownL2 ownL3" % t, O_L + 40 * t, ub(t)
        cp(T.LF[Y, 0, :, :], LAND[Y, :, o:o + 16], x, "LF0")
        cp(T.LF[Y, 1, :, 0:14], LAND[Y, :, o + 16:o + 30], x, "LF1")
        for b in range(2):
            mm(P[5 + b][:, 0:KP], T.LF[Y, b, :, :], T.idn[Y, Y], "LF%d idn" % b, "P%d" % (5 + b))
        cp(T.CF[Y, :], LAND[Y, :, o + 30:o + 33], x, "CF")
        cp(T.OFF[:, 0:KP], P[5][:, 0:KP], "P5", "OF0")
        mm(P[2][0:24, 0:KP], T.CF[Y, :], T.idn[Y, Y], "CF idn", "P2")
        wk = wkeys(t)
        H = BL // 4

        def ga(k, e):
            cp(W[:, u + H * k:u + H * (k + 1)], W[:, 0:u].indirect(T.OFF[:, 28 * k:28 * k + 28]), "OF%d " % (k // 4) + wk, "u%d" % k, e)

        def sc(k):
            scan(T.SC[:, H * k:H * (k + 1)], T.SP[:, k // 4, :], W[:, u + H * k:u + H * (k + 1)], 0.0, mul, add, "SP u%d" % k, "SC%d" % k)

        def theta(G):
            for s in range(2):
                op("a", lambda: a.activation(P[G][:, KP * s:KP * s + KP], T.XS[:, KP * G:KP * G + KP], F.Identity, bias=0.045,
                                             scale=(2 * s - 1) / LCM), "XS%d" % G, "P%d" % G)

        def compare(G):
            for m in range(5):
                for s in range(2):
                    q = 10 * G + 5 * s + m
                    b = q // 16
                    tt(T.CMP[:, KP * q:KP * q + KP], W[:, u + BL * b + q % 16:u + BL * (b + 1):16], P[G][:, KP * s:KP * s + KP], A.is_le,
                       "P%d" % G, "cm%d" % q)
                for s in range(2):
                    q = 10 * G + 5 * s + m
                    mm(P[5][Y, 5 * G + m:120:15], T.CMP[:, KP * q:KP * q + KP], T.gb[:, 8 * (1 - s):8 * (1 - s) + 8], "cm%d gb0 gb1" % q, "P5",
                       s == 0, s == 1)

        ga(1, "a")
        ga(0, "v")
        cp(T.OFF[:, KP:2 * KP], P[6][:, 0:KP], "P6", "OF1")
        cp(T.C1[0:24, :], P[2][0:24, 0:KP], "P2", "C1", "a")
        for G in range(3):
            mm(P[7][:, KP * G:KP * G + KP], T.selc[0:24, 128 * G:128 * G + 128], T.C1[0:24, :], "C1 selc", "P7")
        for k in (2, 3, 4):
            ga(k, "a")
        for k in range(4):
            sc(k)
        S0, S1 = "SC0 SC1 SC2 SC3 ", "SC4 SC5 SC6 SC7 "
        tt(T.XS[:, 0:KP], T.SC[:, 9:BL:16], P[7][:, 0:KP], mul, S0 + "P7", "XS0")
        theta(0)
        for k in (5, 6, 7):
            ga(k, "a")
        sc(4)
        if t > 0:
            tt(T.BS[0:80, 0:32], P[3][0:80, 0:32], T.BS[0:80, 0:32], add, "P3 BS0", "BS0")
            tt(T.BS[:, 64:84], P[4][:, 0:20], T.BS[:, 64:84], add, "P4 BS1", "BS1")
        compare(0)
        for k in (5, 6, 7):
            sc(k)
        tt(T.XS[:, 2 * KP:3 * KP], T.SC[:, BL + 13:2 * BL:16], P[7][:, 2 * KP:3 * KP], mul, S1 + "P7", "XS2")
        theta(2)
        tt(T.XS[:, 3 * KP:4 * KP], T.SC[:, 15:BL:16], T.SC[:, BL + 3:2 * BL:16], add, S0 + S1, "XS3")
        tt(T.XS[:, KP:2 * KP], T.XS[:, 3 * KP:4 * KP], P[7][:, KP:2 * KP], mul, "XS3 P7", "XS1")
        theta(1)
        compare(2)
        compare(1)
        cp(T.VSND[Y, t, 0:120], P[5][Y, 0:120], "P5", "VSND")
        votes_out(t, "x%d" % (3 + t))
        cp(LAND[Y, me, O_V + 16 * t:O_V + 16 * t + 15], T.VSND[Y, t, 15 * me:15 * me + 15], "VSND own", "ownV")
        if t < 2:
            for k in (3, 4):
                mm(P[k][:, :], T.idn[:, :], T.tab[:, 512 * k:512 * k + 512], "tab_%d idn" % k, "P%d" % k, True, False)

    def choose(t):
        o = O_V + 16 * t
        cp(T.VF[Y, :], LAND[Y, :, o:o + 15], "x%d ownV" % (3 + t), "VF")
        tt(T.VA[Y, 0:60], T.VF[Y, 0:60], T.VF[Y, 60:120], add, "VF", "VA0")
        tt(T.VA[Y, 60:90], T.VA[Y, 0:30], T.VA[Y, 30:60], add, "VA0", "VA1")
        tt(T.TT[Y, :, 0, :], T.VA[Y, 60:75], T.VA[Y, 75:90], add, "VA1", "TT0")
        ts(T.TT[Y, :, 1, :], T.TT[Y, :, 0, :], 255, A.bitwise_and, "TT0", "TT1")
        tt(T.OK[Y, :], T.TT[Y, :, :, :], T.TH[Y, :], A.is_ge, "TT0 TT1 TH", "OK")
        scan(T.TF[Y, ::-1], T.k5[Y, :], T.OK[Y, ::-1], 0.0, mul, A.max, "OK k5", TFK)
        tt(T.GO[Y, 0:3], T.TF[Y, 0::10], T.TF[Y, 5::10], A.max, "TF", "GO")
        deps("v", ["GO"], ["V"])
        deps("a", [], ["V"])
        for G in range(3):
            ts(T.TF[Y, 10 * G:10 * G + 5], T.TF[Y, 10 * G:10 * G + 5], T.TF[Y, 10 * G + 5:10 * G + 6], A.is_gt, "TF", "TF%d" % G)
        for G in range(3):
            sca(T.V[Y, 10 * G:10 * G + 10, 4:6], T.C2[Y, 10 * G:10 * G + 10, :], T.GO[Y, G:G + 1], "C20 C21 GO", "")
        if t == 2:
            for r in range(2):
                tt(T.QM[Y, 30 * r:30 * r + 30], T.DK[Y, r, :, :], T.TF[Y, :], mul, "DK DKb" + TFK, "QM%d" % r)
        for r in range(4):
            tt(T.V[Y, 0:30, r], T.C4[Y, r, :], T.TF[Y, :], mul, "C4%d" % r + TFK, "")
        if t == 2:
            scan(T.QS[Y, 0:60], T.k10[Y, :], T.QM[Y, 0:60], 0.0, mul, add, "QM0 QM1 k10", "QS0 QS1")
            tt(T.V[Y, 0:30, 9], T.C4[Y, 4, :], T.TF[Y, :], mul, "C44" + TFK, "")
            for h in range(6):
                sca(T.V[Y, 5 * h:5 * h + 5, 8], T.VA7[Y, 5 * h:5 * h + 5], T.TF[Y, 5 * h:5 * h + 1], "VA7" + TFK, "")
            for r in range(2):
                for G in range(3):
                    j = 30 * r + 10 * G + 9
                    ts(T.V[Y, 10 * G:10 * G + 10, 6 + r], T.VAL[Y, 10 * G:10 * G + 10], T.QS[Y, j:j + 1], mul, "QS0" + VK, "")
        done("V")
        done("Va", "a")
        for k in range(4):
            mm(P[5 + k // 2][:, KP * (k % 2):KP * (k % 2) + KP], T.V[Y, 8 * k:8 * k + 8, :], T.idb[Y, Y], "V Va idb", "P%d" % (5 + k // 2))
        cp(T.VS[:, 0:224], P[5][:, 0:224], "P5", "VS0", "a")
        if t < 2:
            tt(T.QM[Y, 0:30], T.DQ[Y, 0, :, :], T.TF[Y, :], mul, "DQ0 DQ1 DQ2 DQ3" + TFK, "QM0")
            scan(T.QS[Y, 0:30], T.k10[Y, 0:30], T.QM[Y, 0:30], 0.0, mul, add, "QM0 k10", "QS0")
        cp(T.VS[:, 224:448], P[6][:, 0:224], "P6", "VS1")
        if t < 2:
            ts(LAND[Y, me, O_M + 8 * t:O_M + 8 * t + 3], T.QS[Y, 9:30:10], 32768.0, add, "QS0 own", "ownM")
            bcast(O_M + 8 * t, 3, "x%d" % (6 + t), "ownM")
        cp(T.DW[:, :].indirect(T.ofs[:, :]), T.VS[:, :], "VS0 VS1 ofs DW", "DW")

    def new_tables(t):
        for k in (0, 3, 1, 4, 2):
            mm(P[k][:, :], T.bsel[:, :, :], T.DW[:, 512 * k:512 * k + 512], "DW bse0 bse1", "P%d" % k, k < 3, True)
        for k in (0, 3, 1, 4, 2):
            col = T.tab[:, 512 * k:512 * k + 512]
            if k < 3:
                tt(col, T.tab0[:, 512 * k:512 * k + 512] if t == 0 else col, P[k][:, :], add, "P%d tab_%d" % (k, k), "tab_%d" % k)
            else:
                cp(col, P[k][:, :], "P%d" % k, "tab_%d" % k, "a")

    first_ends(0)
    ms(T.SP[:, :, :], 1.0, "SP")
    for t in range(3):
        chains(t)
        meeting(t)
        if t == 0:
            consts()
        else:
            update(t - 1)
        worker(t)
        prepare(t)
        choose(t)
        if t < 2:
            new_tables(t)

    turn_over(2, 2)
    ends(2)
    tt(T.BT[0:80, 0:64], P[3][0:80, 0:64], T.BS[0:80, 0:64], add, "P3 BS0 BS2", "BT0")
    cp(LAND[0:80, me, O_F:O_F + 64], T.BT[0:80, 0:64], "BT0 own", "ownF")
    bcast(O_F, 64, "x8", "ownF")
    mm(P[5][0:126, 0:16], T.EN[Y, :, :], T.m16[Y, :], "EN0 EN1 EN2 m16", "P5")
    tt(T.BT[:, 64:84], P[4][:, 0:20], T.BS[:, 64:84], add, "P4 BS1", "BT1")
    cp(LAND[0:126, me, O_P + 20:O_P + 36], P[5][0:126, 0:16], "P5 own", "ownE")
    cp(LAND[:, me, O_P:O_P + 20], T.BT[:, 64:84], "BT1 own", "ownP")
    hc = helper_of(core, T, topo)
    deps("p", ["ownP", "ownE"], [])
    ap = LAND[:, me, O_P:O_P + 36]
    g.remote_dma_fused([RemoteDMATransfer(dst_ids=[to(hc, topo)], dma_engine_mask=topo.mask(core, hc), remote_sem=T.sem.hand, src=ap, dst=ap)],
                       local_sem=T.sem.sent)
    sent[0] += len(topo.engines(core, hc))
    lastw["x9"] = ("x9", len(topo.engines(hc, core)) * len(peers))
    for l in (1, 0):
        for b in range(2):
            j = 2 * l + b
            cp(T.LF[0:80, j, :, :], LAND[0:80, :, O_F + 16 * j:O_F + 16 * j + 16], "x8 ownF", "LF%d" % j)
            mm(P[6 + l][:, 80 * b:80 * b + 80], T.LF[0:80, j, :, :], T.idn[0:80, 0:80], "LF%d idn" % j, "P%d" % (6 + l))
    for l in (1, 0):
        cp(T.OFF[:, 160 * l:160 * l + 160], P[6 + l][:, 0:160], "P%d" % (6 + l), "OF0 OF1" if l == 0 else "OF2")
    wk = wkeys(2) + " N2 u0 u1 u2 u3 u4 u5 u6 u7"
    cuts = (0, 16, 40, 72, 104, 136, 160)
    for k in range(6):
        c0, c1 = cuts[k], cuts[k + 1]
        cp(T.Y2[:, 16 * c0:16 * c1], W[:, :].indirect(T.OFF[:, 160 + c0:160 + c1]), "OF2 " + wk, "Y2%d" % k, "a")
        tt(T.YF[:, 16 * c0:16 * c1], W[:, :].indirect(T.OFF[:, c0:c1]), T.Y2[:, 16 * c0:16 * c1], add, "OF0 Y2%d " % k + wk, "YF%d" % k)
        dma("s", T.yf[:, 16 * c0:16 * c1], T.YF[:, 16 * c0:16 * c1], "dout", "YF%d" % k, "")
    cp(T.PFI[:, :], LAND[:, :, O_P:O_P + 20], "x9 ownP", "PFI")
    cp(T.EFI[0:126, :], LAND[0:126, :, O_P + 20:O_P + 36], "x9 ownE", "EFI")
    for b in range(2):
        mm(P[2][0:80, 128 * b:128 * b + 128], T.PFI[:, 80 * b:80 * b + 80], T.idn[:, :], "PFI idn", "P2")
    mm(P[5][:, 0:120], T.EFI[0:126, :], T.id21[0:126, :, 0:20], "EFI id21", "P5")
    tt(T.YP[0:80, :], P[2][0:80, 0:256], T.PR[0:80, :], add, "P2 PR", "YP")
    cp(T.YT[:, :], P[5][:, 0:120], "P5", "YT", "a")
    for b in range(2):
        dma("s", T.yp[4 * b:4 * b + 4, :], T.YP[0:80, 128 * b:128 * b + 128], "dout", "YP", "")
    dma("a", T.yt[:, :], T.YT[:, :], "dout", "YT", "")
    wait("s", ("dout", dcount["dout"]))
    wait("p", ("sent", sent[0]))
    for e in "vatp":
        wait("s", ("c" + e, cnt[e]))
